import numpy as np
import ml_dtypes


def mxq(x, axis, fmt="e4m3"):
    dtype, down = {"e4m3": (ml_dtypes.float8_e4m3fn, 7), "e5m2": (ml_dtypes.float8_e5m2, 14)}[fmt]
    v = np.moveaxis(np.asarray(x, np.float32).astype(ml_dtypes.bfloat16).astype(np.float64), axis, -1)
    blocks = v.reshape(v.shape[:-1] + (-1, 32))
    amax = np.abs(blocks).max(-1, keepdims=True)
    byte = np.maximum(np.where(amax > 0, np.frexp(amax)[1] - 1 + 127, 0) - down, 1)
    scale = np.exp2(byte - 127.0)
    codes = (blocks / scale).astype(np.float32).astype(dtype).astype(np.float64)
    return np.moveaxis((codes * scale).reshape(v.shape), -1, axis)


WIDE = False


def mx_kscale(k):
    if not WIDE:
        return np.ones(k)
    levels = np.array([10, -10, 5, -5, 0])
    if k % 512:
        return np.exp2(np.random.permutation(np.resize(levels, k // 32))).repeat(32)
    a = np.empty((k // 512, 16))
    for p in range(k // 512):
        a[p, :8] = np.random.permutation(np.resize(levels, 8))
        for g in range(8):
            far = levels[np.abs(levels - a[p, g]) >= 10]
            a[p, g + 8] = far[np.random.randint(len(far))]
    return np.exp2(a.ravel()).repeat(32)


BF16 = ml_dtypes.bfloat16


def bf(x):
    return np.asarray(x, np.float32).astype(BF16)


def f64(x):
    return np.asarray(x).astype(np.float64)

def planes(Y):
    n, m = Y.shape
    b = f64(bf(Y)).reshape(n // 32, 32, m)
    amax = np.abs(b).max(1)
    byte = np.clip(np.where(amax > 0, np.frexp(amax)[1] - 1 + 127 - 7, 1), 1, 254)
    codes = (b * np.exp2(127.0 - byte)[:, None, :]).reshape(n, m).astype(np.float32).astype(ml_dtypes.float8_e4m3fn).view(np.uint8)
    words = codes.reshape(n // 512, 128, 4, m).transpose(0, 1, 3, 2)
    return np.ascontiguousarray(words), np.ascontiguousarray(byte.astype(np.uint8).reshape(n // 512, 16, m))


P, B = 1536, 1024


def weighted_derivative():
    theta = (np.arange(P) + 0.5) * np.pi / P
    x, sn = np.cos(theta), np.sin(theta)
    sg = (-1.0) ** np.arange(P)
    gap = x[:, None] - x[None, :] + np.eye(P)
    G = sg[:, None] * sg[None, :] * sn[None, :] / (P * gap)
    np.fill_diagonal(G, x / (2 * P * sn))
    return G

def setup_inputs():
    s = mx_kscale(P)
    amp = np.exp(0.8 * np.random.randn(P))
    D = bf(weighted_derivative() * (amp * s)[None, :])
    h = bf(np.random.randn(P, B) / s[:, None])
    p = bf(amp * s)
    return {"D": D, "h": h, "p": p}

def reference(D, h, p):
    D, h, p = f64(D), f64(h), f64(p)
    slope = mxq(D, 1, "e4m3") @ mxq(h, 0, "e4m3")
    u = p[:, None] * h
    y = -(u * slope)
    Y = y.reshape(P, B)
    words, scales = planes(Y)
    return y, words, scales

@@ -1,0 +1,292 @@
+from contextlib import ExitStack
+
+import concourse.mybir as mybir
+from concourse.masks import make_identity
+
+POINTS, FIELDS = 1536, 1024
+FLOPS = 2 * POINTS * POINTS * FIELDS
+
+F32 = mybir.dt.float32
+BF16 = mybir.dt.bfloat16
+U32 = mybir.dt.uint32
+I32 = mybir.dt.int32
+U8 = mybir.dt.uint8
+FP8X4 = mybir.dt.float8_e4m3fn_x4
+MULT = mybir.AluOpType.mult
+ADD = mybir.AluOpType.add
+
+P = 128
+PACK = 4
+GROUP = P * PACK
+GROUPS = POINTS // GROUP
+HALF = 512
+RUN = 4
+
+
+def tile_chebyshev_self_advection_g2_kernel(tc, D, h, p, out_0, out_1, out_2):
+    nc = tc.nc
+    with ExitStack() as ctx:
+        keep = ctx.enter_context(tc.tile_pool(name="keep", bufs=1))
+        stage = ctx.enter_context(tc.tile_pool(name="stage", bufs=3))
+        psum = ctx.enter_context(tc.psum_pool(name="psum", bufs=1))
+        ctx.enter_context(tc.manual_schedule())
+
+        h_raw, h_packed, h_codes, h_scales = {}, {}, {}, {}
+        d_raw, d_bank, d_packed, d_codes, d_scales = {}, {}, {}, {}, {}
+        acc, y, y_packed, y_codes, y_scales = {}, {}, {}, {}, {}
+        words_out = out_1.rearrange("g p m t -> g p (m t)").bitcast(I32)
+        scales_out = out_2.bitcast(I32)
+
+        def load_h(half, g):
+            h_raw[half, g] = keep.tile([P, PACK, HALF], BF16, name="h_raw_%d_%d" % (half, g), align_bytes=64)
+            rows = h[GROUP * g : GROUP * (g + 1), HALF * half : HALF * (half + 1)]
+            nc.sync.dma_start(out=h_raw[half, g][:], in_=rows.rearrange("(p t) n -> p t n", t=PACK))
+
+        def load_d(pair):
+            g, q = divmod(pair, 2)
+            d_raw[pair] = keep.tile([P, 2, POINTS], BF16, name="d_raw_%d" % pair, align_bytes=64)
+            rows = D[GROUP * g : GROUP * (g + 1), :].rearrange("(m t) k -> m t k", t=PACK)
+            nc.sync.dma_start(out=d_raw[pair][:], in_=rows[:, 2 * q : 2 * q + 2, :])
+
+        def interleave(copy, packed, raw, lo, hi):
+            copy(
+                out=packed[:, lo:hi, :].rearrange("p (c i) t -> p c t i", i=RUN),
+                in_=raw[:, :, lo:hi].rearrange("p t (c i) -> p c t i", i=RUN),
+            )
+
+        def pack_h(half, g, split):
+            h_packed[half, g] = stage.tile([P, HALF, PACK], BF16, name="h_packed", align_bytes=64)
+            if split > 0:
+                interleave(nc.vector.tensor_copy, h_packed[half, g], h_raw[half, g], 0, split)
+            if split < HALF:
+                interleave(nc.scalar.copy, h_packed[half, g], h_raw[half, g], split, HALF)
+
+        def quantize_h(half, g):
+            h_codes[half, g] = keep.tile([P, HALF], U32, name="h_codes_%d_%d" % (half, g), align_bytes=64)
+            h_scales[half, g] = keep.tile([P, HALF], U8, name="h_scales_%d_%d" % (half, g), align_bytes=64)
+            nc.vector.quantize_mx(
+                out=h_codes[half, g][:].bitcast(FP8X4),
+                scales=h_scales[half, g][:],
+                in_=h_packed[half, g][:].rearrange("p n t -> p (n t)"),
+            )
+
+        def turn_d(pair, c):
+            words = d_raw[pair][:].rearrange("p a k -> p (a k)").bitcast(F32)
+            bank = psum.tile([P, 2, 2, P], F32, name="d_bank", bufs=3)
+            for a in range(2):
+                for u in range(2):
+                    base = a * POINTS // 2 + c * GROUP // 2
+                    nc.tensor.transpose(bank[:, a, u, :], words[:, base + u : base + GROUP // 2 : 2], identity[:])
+            d_bank[pair, c] = bank
+
+        def pack_d(pair, c):
+            d_packed[pair, c] = stage.tile([P, 2 * GROUP], BF16, name="d_packed", bufs=4, align_bytes=64)
+            nc.scalar.copy(
+                out=d_packed[pair, c][:].bitcast(F32).rearrange("p (a m u) -> p a m u", a=2, u=2),
+                in_=d_bank[pair, c][:].rearrange("p a u m -> p a m u"),
+            )
+
+        def quantize_d(pair, c):
+            d_codes[pair, c] = keep.tile([P, 2 * P], U32, name="d_codes_%d_%d" % (pair, c), align_bytes=64)
+            d_scales[pair, c] = keep.tile([P, 2 * P], U8, name="d_scales_%d_%d" % (pair, c), align_bytes=64)
+            nc.vector.quantize_mx(
+                out=d_codes[pair, c][:].bitcast(FP8X4), scales=d_scales[pair, c][:], in_=d_packed[pair, c][:]
+            )
+
+        def multiply(pair, half, a, c, lo=0, hi=HALF):
+            if c == 0:
+                acc[pair, half, a, lo] = psum.tile([P, hi - lo], F32, name="acc", bufs=5)
+            cols = slice(a * P, (a + 1) * P)
+            nc.tensor.matmul_mx(
+                out=acc[pair, half, a, lo][:],
+                lhsT=d_codes[pair, c][:, cols].bitcast(FP8X4),
+                lhsT_scale=d_scales[pair, c][:, cols],
+                rhs=h_codes[half, c][:, lo:hi].bitcast(FP8X4),
+                rhs_scale=h_scales[half, c][:, lo:hi],
+                start=(c == 0),
+                stop=(c == GROUPS - 1),
+            )
+
+        def advect(pair, half, a, lo=0, hi=HALF):
+            g, q = divmod(pair, 2)
+            t = 2 * q + a
+            if t == 0:
+                y[g, half, lo] = stage.tile([P, PACK, hi - lo], F32, name="y", bufs=4, align_bytes=64)
+            nc.vector.scalar_tensor_tensor(
+                out=y[g, half, lo][:, t, :],
+                in0=h_raw[half, g][:, t, lo:hi],
+                scalar=minus_p[:, g, t : t + 1],
+                in1=acc[pair, half, a, lo][:],
+                op0=MULT,
+                op1=MULT,
+            )
+
+        def store_y(g, half, t0, t1, lo=0, hi=HALF):
+            rows = out_0[GROUP * g : GROUP * (g + 1), HALF * half + lo : HALF * half + hi]
+            nc.sync.dma_start(
+                out=rows.rearrange("(p t) n -> p t n", t=PACK)[:, t0:t1, :], in_=y[g, half, lo][:, t0:t1, :]
+            )
+
+        def pack_y(g, half, split, lo=0, hi=HALF):
+            y_packed[g, half, lo] = stage.tile([P, hi - lo, PACK], BF16, name="y_packed", align_bytes=64)
+            if split > 0:
+                interleave(nc.vector.tensor_copy, y_packed[g, half, lo], y[g, half, lo], 0, split)
+            if split < hi - lo:
+                interleave(nc.scalar.copy, y_packed[g, half, lo], y[g, half, lo], split, hi - lo)
+
+        def quantize_y(g, half, lo=0, hi=HALF):
+            y_codes[g, half, lo] = stage.tile([P, hi - lo], U32, name="y_codes", align_bytes=64)
+            if half == 0 and lo == 0:
+                y_scales[g] = keep.tile([P, FIELDS], U8, name="y_scales_%d" % g, align_bytes=64)
+            nc.vector.quantize_mx(
+                out=y_codes[g, half, lo][:].bitcast(FP8X4),
+                scales=y_scales[g][:, HALF * half + lo : HALF * half + hi],
+                in_=y_packed[g, half, lo][:].rearrange("p n t -> p (n t)"),
+            )
+
+        def store_codes(g, half, lo=0, hi=HALF):
+            nc.sync.dma_start(
+                out=words_out[g, :, HALF * half + lo : HALF * half + hi], in_=y_codes[g, half, lo][:].bitcast(I32)
+            )
+
+        def store_scales(g, queues):
+            for quad in range(4):
+                queues[quad % len(queues)].dma_start(
+                    out=scales_out[g, 4 * quad : 4 * quad + 4, :],
+                    in_=y_scales[g][32 * quad : 32 * quad + 4, :].bitcast(I32),
+                )
+
+        p_raw = keep.tile([P, GROUPS, PACK], BF16, name="p_raw")
+        minus_p = keep.tile([P, GROUPS, PACK], F32, name="minus_p")
+        identity = keep.tile([P, P], F32, name="identity")
+
+        load_d(0); load_h(0, 0); load_h(0, 1); load_d(1); load_h(0, 2); load_h(1, 0); load_d(2)
+        load_h(1, 1); load_h(1, 2); load_d(3); load_d(4); load_d(5)
+        nc.gpsimd.dma_start(out=p_raw[:], in_=p.rearrange("(g p t) -> p g t", p=P, t=PACK))
+        make_identity(nc, identity[:])
+        nc.gpsimd.tensor_scalar(out=minus_p[:], in0=p_raw[:], scalar1=-1.0, scalar2=0.0, op0=MULT, op1=ADD)
+
+        def mm(pair, half, lo=0, hi=HALF):
+            for a in range(2):
+                for c in range(3):
+                    multiply(pair, half, a, c, lo, hi)
+
+        def turn(pair):
+            for c in range(3):
+                turn_d(pair, c)
+
+        def ready_d(pair):
+            for c in range(3):
+                pack_d(pair, c)
+                quantize_d(pair, c)
+
+        def finish(pair, half):
+            g, q = divmod(pair, 2)
+            advect(pair, half, 0)
+            advect(pair, half, 1)
+            store_y(g, half, 2 * q, 2 * q + 2)
+
+        turn(0)
+        pack_d(0, 0)
+        pack_h(0, 0, 336)
+        quantize_d(0, 0)
+        quantize_h(0, 0)
+        pack_d(0, 1)
+        pack_h(0, 1, 384)
+        pack_d(0, 2)
+        quantize_d(0, 1)
+        quantize_h(0, 1)
+        quantize_d(0, 2)
+        for c in range(2):
+            for a in range(2):
+                multiply(0, 0, a, c)
+        turn(1)
+        pack_h(0, 2, 336)
+        quantize_h(0, 2)
+        pack_h(1, 0, 256)
+        pack_d(1, 0)
+        quantize_h(1, 0)
+        quantize_d(1, 0)
+        pack_d(1, 1)
+        quantize_d(1, 1)
+        pack_d(1, 2)
+        for a in range(2):
+            multiply(0, 0, a, 2)
+        turn(2)
+        advect(0, 0, 0)
+        quantize_d(1, 2)
+        advect(0, 0, 1)
+        store_y(0, 0, 0, 2)
+        pack_d(2, 0)
+        pack_d(2, 1)
+        pack_d(2, 2)
+        pack_h(1, 1, 256)
+        quantize_d(2, 0)
+        quantize_d(2, 1)
+        quantize_d(2, 2)
+        mm(1, 0)
+        turn(3)
+        advect(1, 0, 0)
+        quantize_h(1, 1)
+        advect(1, 0, 1)
+        store_y(0, 0, 2, 4)
+        pack_d(3, 0)
+        pack_d(3, 1)
+        pack_d(3, 2)
+        pack_h(1, 2, 192)
+        quantize_d(3, 0)
+        quantize_d(3, 1)
+        quantize_d(3, 2)
+        mm(2, 0)
+        pack_y(0, 0, 0)
+        advect(2, 0, 0)
+        advect(2, 0, 1)
+        store_y(1, 0, 0, 2)
+        quantize_h(1, 2)
+        mm(3, 0)
+        turn(4)
+        finish(3, 0)
+        quantize_y(0, 0); store_codes(0, 0)
+        ready_d(4)
+        pack_y(1, 0, 0)
+        mm(0, 1)
+        finish(0, 1)
+        mm(1, 1)
+        turn(5)
+        advect(1, 1, 0)
+        quantize_y(1, 0)
+        advect(1, 1, 1)
+        store_y(0, 1, 2, 4)
+        store_codes(1, 0)
+        ready_d(5)
+        pack_y(0, 1, 0)
+        mm(2, 1)
+        finish(2, 1)
+        mm(3, 1)
+        advect(3, 1, 0)
+        quantize_y(0, 1)
+        advect(3, 1, 1)
+        store_y(1, 1, 2, 4)
+        store_codes(0, 1); store_scales(0, [nc.sync])
+        pack_y(1, 1, 0)
+        last = [(0, 0), (0, 256), (1, 0), (1, 256)]
+        for i, (half, lo) in enumerate(last):
+            hi = lo + 256
+            mm(4, half, lo, hi)
+            mm(5, half, lo, hi)
+            advect(4, half, 0, lo, hi)
+            advect(4, half, 1, lo, hi)
+            if i == 3:
+                store_y(2, half, 0, 2, lo, hi)
+            if i == 1:
+                quantize_y(1, 1); store_codes(1, 1); store_scales(1, [nc.sync])
+            if i > 1:
+                quantize_y(2, last[i - 2][0], last[i - 2][1], last[i - 2][1] + 256)
+                store_codes(2, last[i - 2][0], last[i - 2][1], last[i - 2][1] + 256)
+            advect(5, half, 0, lo, hi)
+            advect(5, half, 1, lo, hi)
+            store_y(2, half, 2 if i == 3 else 0, 4, lo, hi)
+            if i == 3:
+                quantize_y(2, 1, 0, 256); store_codes(2, 1, 0, 256)
+            pack_y(2, half, 160 if i == 3 else 0, lo, hi)
+        quantize_y(2, 1, 256, 512); store_codes(2, 1, 256, 512); store_scales(2, [nc.scalar, nc.sync])

@@ -111,9 +111,21 @@ def tile_chebyshev_self_advection_g2_kernel(tc, D, h, p, out_0, out_1, out_2):
             g, q = divmod(pair, 2)
             t = 2 * q + a
             if t == 0:
-                y[g, half, lo] = stage.tile([P, PACK, hi - lo], F32, name="y", bufs=4, align_bytes=64)
+                y[g, half, lo] = stage.tile([P, PACK, hi - lo], F32, name="y", bufs=5, align_bytes=64)
             nc.vector.scalar_tensor_tensor(
                 out=y[g, half, lo][:, t, :],
+                in0=h_raw[half, g][:, t, lo:hi],
+                scalar=minus_p[:, g, t : t + 1],
+                in1=acc[pair, half, a, lo][:],
+                op0=MULT,
+                op1=MULT,
+            )
+
+        def advect_part(pair, half, a, lo, hi):
+            g, q = divmod(pair, 2)
+            t = 2 * q + a
+            nc.vector.scalar_tensor_tensor(
+                out=y[g, half, 0][:, t, lo:hi],
                 in0=h_raw[half, g][:, t, lo:hi],
                 scalar=minus_p[:, g, t : t + 1],
                 in1=acc[pair, half, a, lo][:],
@@ -136,11 +148,11 @@ def tile_chebyshev_self_advection_g2_kernel(tc, D, h, p, out_0, out_1, out_2):
 
         def quantize_y(g, half, lo=0, hi=HALF):
             y_codes[g, half, lo] = stage.tile([P, hi - lo], U32, name="y_codes", align_bytes=64)
-            if half == 0 and lo == 0:
-                y_scales[g] = keep.tile([P, FIELDS], U8, name="y_scales_%d" % g, align_bytes=64)
+            if half == 0 and lo == 0 and g != 1:
+                y_scales[g // 2] = keep.tile([P, FIELDS], U8, name="y_scales_%d" % (g // 2), align_bytes=64)
             nc.vector.quantize_mx(
                 out=y_codes[g, half, lo][:].bitcast(FP8X4),
-                scales=y_scales[g][:, HALF * half + lo : HALF * half + hi],
+                scales=y_scales[g // 2][4 * (g % 2) :, HALF * half + lo : HALF * half + hi],
                 in_=y_packed[g, half, lo][:].rearrange("p n t -> p (n t)"),
             )
 
@@ -149,19 +161,19 @@ def tile_chebyshev_self_advection_g2_kernel(tc, D, h, p, out_0, out_1, out_2):
                 out=words_out[g, :, HALF * half + lo : HALF * half + hi], in_=y_codes[g, half, lo][:].bitcast(I32)
             )
 
-        def store_scales(g, queues):
+        def store_scales(g0, g1, queues):
             for quad in range(4):
                 queues[quad % len(queues)].dma_start(
-                    out=scales_out[g, 4 * quad : 4 * quad + 4, :],
-                    in_=y_scales[g][32 * quad : 32 * quad + 4, :].bitcast(I32),
+                    out=scales_out[g0:g1, 4 * quad : 4 * quad + 4, :],
+                    in_=y_scales[g0 // 2][32 * quad : 32 * quad + 4 * (g1 - g0), :].bitcast(I32),
                 )
 
         p_raw = keep.tile([P, GROUPS, PACK], BF16, name="p_raw")
         minus_p = keep.tile([P, GROUPS, PACK], F32, name="minus_p")
         identity = keep.tile([P, P], F32, name="identity")
 
-        load_d(0); load_h(0, 0); load_h(0, 1); load_d(1); load_h(0, 2); load_h(1, 0); load_d(2)
-        load_h(1, 1); load_h(1, 2); load_d(3); load_d(4); load_d(5)
+        load_h(0, 0); load_d(0); load_h(0, 1); load_d(1); load_h(0, 2); load_d(2); load_h(1, 0); load_d(3)
+        load_h(1, 1); load_h(1, 2); load_d(4); load_d(5)
         nc.gpsimd.dma_start(out=p_raw[:], in_=p.rearrange("(g p t) -> p g t", p=P, t=PACK))
         make_identity(nc, identity[:])
         nc.gpsimd.tensor_scalar(out=minus_p[:], in0=p_raw[:], scalar1=-1.0, scalar2=0.0, op0=MULT, op1=ADD)
@@ -186,107 +198,125 @@ def tile_chebyshev_self_advection_g2_kernel(tc, D, h, p, out_0, out_1, out_2):
             advect(pair, half, 1)
             store_y(g, half, 2 * q, 2 * q + 2)
 
-        turn(0)
-        pack_d(0, 0)
+        warm_in = keep.tile([P, GROUP], BF16, name="warm_in", align_bytes=64)
+        warm_codes = keep.tile([P, P], U32, name="warm_codes", align_bytes=64)
+        warm_scales = keep.tile([P, P], U8, name="warm_scales", align_bytes=64)
+        nc.vector.memset(warm_in[:], 1.0)
+        nc.vector.quantize_mx(out=warm_codes[:].bitcast(FP8X4), scales=warm_scales[:], in_=warm_in[:])
+
+        def warm(n):
+            bank = psum.tile([P, P], F32, name="acc", bufs=5)
+            for i in range(n):
+                nc.tensor.matmul_mx(out=bank[:], lhsT=warm_codes[:].bitcast(FP8X4), lhsT_scale=warm_scales[:],
+                                    rhs=warm_codes[:].bitcast(FP8X4), rhs_scale=warm_scales[:], start=True, stop=True)
+
+        warm(32)
         pack_h(0, 0, 336)
-        quantize_d(0, 0)
         quantize_h(0, 0)
+        turn(0)
+        warm(4)
+        pack_d(0, 0)
+        pack_h(0, 1, 400)
+        quantize_d(0, 0)
         pack_d(0, 1)
-        pack_h(0, 1, 384)
+        quantize_h(0, 1)
         pack_d(0, 2)
         quantize_d(0, 1)
-        quantize_h(0, 1)
         quantize_d(0, 2)
-        for c in range(2):
-            for a in range(2):
-                multiply(0, 0, a, c)
+        for a in range(2):
+            multiply(0, 0, a, 0)
         turn(1)
-        pack_h(0, 2, 336)
-        quantize_h(0, 2)
-        pack_h(1, 0, 256)
+        for a in range(2):
+            multiply(0, 0, a, 1)
         pack_d(1, 0)
-        quantize_h(1, 0)
+        pack_h(0, 2, 400)
         quantize_d(1, 0)
         pack_d(1, 1)
-        quantize_d(1, 1)
+        quantize_h(0, 2)
         pack_d(1, 2)
+        quantize_d(1, 1)
+        quantize_d(1, 2)
+        for a in range(2):
+            multiply(1, 0, a, 0)
+        turn(2)
         for a in range(2):
             multiply(0, 0, a, 2)
-        turn(2)
-        advect(0, 0, 0)
-        quantize_d(1, 2)
-        advect(0, 0, 1)
-        store_y(0, 0, 0, 2)
+        for c in range(1, 3):
+            for a in range(2):
+                multiply(1, 0, a, c)
         pack_d(2, 0)
         pack_d(2, 1)
         pack_d(2, 2)
-        pack_h(1, 1, 256)
+        pack_h(1, 0, 256)
         quantize_d(2, 0)
+        advect(0, 0, 0)
         quantize_d(2, 1)
+        advect(0, 0, 1)
         quantize_d(2, 2)
-        mm(1, 0)
+        store_y(0, 0, 0, 2)
         turn(3)
         advect(1, 0, 0)
-        quantize_h(1, 1)
+        quantize_h(1, 0)
         advect(1, 0, 1)
         store_y(0, 0, 2, 4)
         pack_d(3, 0)
         pack_d(3, 1)
         pack_d(3, 2)
-        pack_h(1, 2, 192)
+        pack_h(1, 1, 256)
         quantize_d(3, 0)
         quantize_d(3, 1)
         quantize_d(3, 2)
         mm(2, 0)
-        pack_y(0, 0, 0)
+        pack_h(1, 2, 192)
         advect(2, 0, 0)
+        quantize_h(1, 1)
         advect(2, 0, 1)
         store_y(1, 0, 0, 2)
         quantize_h(1, 2)
         mm(3, 0)
         turn(4)
         finish(3, 0)
-        quantize_y(0, 0); store_codes(0, 0)
         ready_d(4)
-        pack_y(1, 0, 0)
+        pack_y(0, 0, 0)
         mm(0, 1)
         finish(0, 1)
+        quantize_y(0, 0); store_codes(0, 0)
+        pack_y(1, 0, 0)
         mm(1, 1)
-        turn(5)
-        advect(1, 1, 0)
-        quantize_y(1, 0)
-        advect(1, 1, 1)
-        store_y(0, 1, 2, 4)
-        store_codes(1, 0)
-        ready_d(5)
-        pack_y(0, 1, 0)
+        finish(1, 1)
         mm(2, 1)
-        finish(2, 1)
+        advect(2, 1, 0)
+        quantize_y(1, 0)
+        advect(2, 1, 1)
+        store_codes(1, 0)
+        store_y(1, 1, 0, 2)
+        pack_y(0, 1, 0)
         mm(3, 1)
-        advect(3, 1, 0)
-        quantize_y(0, 1)
-        advect(3, 1, 1)
-        store_y(1, 1, 2, 4)
-        store_codes(0, 1); store_scales(0, [nc.sync])
+        turn(5)
+        finish(3, 1)
+        quantize_y(0, 1); store_codes(0, 1)
+        ready_d(5)
         pack_y(1, 1, 0)
-        last = [(0, 0), (0, 256), (1, 0), (1, 256)]
-        for i, (half, lo) in enumerate(last):
-            hi = lo + 256
-            mm(4, half, lo, hi)
-            mm(5, half, lo, hi)
-            advect(4, half, 0, lo, hi)
-            advect(4, half, 1, lo, hi)
-            if i == 3:
-                store_y(2, half, 0, 2, lo, hi)
-            if i == 1:
-                quantize_y(1, 1); store_codes(1, 1); store_scales(1, [nc.sync])
-            if i > 1:
-                quantize_y(2, last[i - 2][0], last[i - 2][1], last[i - 2][1] + 256)
-                store_codes(2, last[i - 2][0], last[i - 2][1], last[i - 2][1] + 256)
-            advect(5, half, 0, lo, hi)
-            advect(5, half, 1, lo, hi)
-            store_y(2, half, 2 if i == 3 else 0, 4, lo, hi)
-            if i == 3:
-                quantize_y(2, 1, 0, 256); store_codes(2, 1, 0, 256)
-            pack_y(2, half, 160 if i == 3 else 0, lo, hi)
-        quantize_y(2, 1, 256, 512); store_codes(2, 1, 256, 512); store_scales(2, [nc.scalar, nc.sync])
+        mm(4, 0)
+        finish(4, 0)
+        mm(5, 0)
+        advect(5, 0, 0)
+        advect(5, 0, 1)
+        store_y(2, 0, 2, 4)
+        quantize_y(1, 1)
+        store_codes(1, 1); store_scales(0, 2, [nc.sync])
+        pack_y(2, 0, 0)
+        mm(4, 1)
+        finish(4, 1)
+        mm(5, 1, 0, 256)
+        advect_part(5, 1, 0, 0, 256)
+        advect_part(5, 1, 1, 0, 256)
+        y_packed[2, 1, 0] = stage.tile([P, HALF, PACK], BF16, name="y_packed", align_bytes=64)
+        interleave(nc.scalar.copy, y_packed[2, 1, 0], y[2, 1, 0], 0, 256)
+        mm(5, 1, 256, 512)
+        advect_part(5, 1, 0, 256, 512)
+        advect_part(5, 1, 1, 256, 512)
+        store_y(2, 1, 2, 4)
+        quantize_y(2, 0); store_codes(2, 0)
+        interleave(nc.vector.tensor_copy, y_packed[2, 1, 0], y[2, 1, 0], 256, 512)
+        quantize_y(2, 1); store_codes(2, 1); store_scales(2, 3, [nc.scalar, nc.sync])

@@ -54,6 +54,11 @@ def tile_chebyshev_self_advection_g2_kernel(tc, D, h, p, out_0, out_1, out_2):
                 in_=raw[:, :, lo:hi].rearrange("p t (c i) -> p c t i", i=RUN),
             )
 
+        def pack_h_part(copy, half, g, lo, hi):
+            if lo == 0:
+                h_packed[half, g] = stage.tile([P, HALF, PACK], BF16, name="h_packed", align_bytes=64)
+            interleave(copy, h_packed[half, g], h_raw[half, g], lo, hi)
+
         def pack_h(half, g, split):
             h_packed[half, g] = stage.tile([P, HALF, PACK], BF16, name="h_packed", align_bytes=64)
             if split > 0:
@@ -80,18 +85,22 @@ def tile_chebyshev_self_advection_g2_kernel(tc, D, h, p, out_0, out_1, out_2):
             d_bank[pair, c] = bank
 
         def pack_d(pair, c):
-            d_packed[pair, c] = stage.tile([P, 2 * GROUP], BF16, name="d_packed", bufs=4, align_bytes=64)
+            if c < 2:
+                d_packed[pair, c] = stage.tile([P, 2 * GROUP * (c + 1)], BF16, name="d_packed_%d" % c, bufs=2, align_bytes=64)
+            part = d_packed[pair, min(c, 1)][:, 2 * GROUP * (c // 2) : 2 * GROUP * (c // 2 + 1)]
             nc.scalar.copy(
-                out=d_packed[pair, c][:].bitcast(F32).rearrange("p (a m u) -> p a m u", a=2, u=2),
+                out=part.bitcast(F32).rearrange("p (a m u) -> p a m u", a=2, u=2),
                 in_=d_bank[pair, c][:].rearrange("p a u m -> p a m u"),
             )
 
-        def quantize_d(pair, c):
-            d_codes[pair, c] = keep.tile([P, 2 * P], U32, name="d_codes_%d_%d" % (pair, c), align_bytes=64)
-            d_scales[pair, c] = keep.tile([P, 2 * P], U8, name="d_scales_%d_%d" % (pair, c), align_bytes=64)
-            nc.vector.quantize_mx(
-                out=d_codes[pair, c][:].bitcast(FP8X4), scales=d_scales[pair, c][:], in_=d_packed[pair, c][:]
-            )
+        def quantize_d(pair, part):
+            width = 2 * P * (part + 1)
+            codes = keep.tile([P, width], U32, name="d_codes_%d_%d" % (pair, part), align_bytes=64)
+            scales = keep.tile([P, width], U8, name="d_scales_%d_%d" % (pair, part), align_bytes=64)
+            nc.vector.quantize_mx(out=codes[:].bitcast(FP8X4), scales=scales[:], in_=d_packed[pair, part][:])
+            for j in range(part + 1):
+                d_codes[pair, part + j] = codes[:, 2 * P * j : 2 * P * (j + 1)]
+                d_scales[pair, part + j] = scales[:, 2 * P * j : 2 * P * (j + 1)]
 
         def multiply(pair, half, a, c, lo=0, hi=HALF):
             if c == 0:
@@ -172,7 +181,7 @@ def tile_chebyshev_self_advection_g2_kernel(tc, D, h, p, out_0, out_1, out_2):
         minus_p = keep.tile([P, GROUPS, PACK], F32, name="minus_p")
         identity = keep.tile([P, P], F32, name="identity")
 
-        load_h(0, 0); load_d(0); load_h(0, 1); load_d(1); load_h(0, 2); load_d(2); load_h(1, 0); load_d(3)
+        load_d(0); load_h(0, 0); load_d(1); load_h(0, 1); load_d(2); load_h(0, 2); load_h(1, 0); load_d(3)
         load_h(1, 1); load_h(1, 2); load_d(4); load_d(5)
         nc.gpsimd.dma_start(out=p_raw[:], in_=p.rearrange("(g p t) -> p g t", p=P, t=PACK))
         make_identity(nc, identity[:])
@@ -210,99 +219,82 @@ def tile_chebyshev_self_advection_g2_kernel(tc, D, h, p, out_0, out_1, out_2):
                 nc.tensor.matmul_mx(out=bank[:], lhsT=warm_codes[:].bitcast(FP8X4), lhsT_scale=warm_scales[:],
                                     rhs=warm_codes[:].bitcast(FP8X4), rhs_scale=warm_scales[:], start=True, stop=True)
 
-        warm(32)
-        pack_h(0, 0, 336)
-        quantize_h(0, 0)
-        turn(0)
-        warm(4)
-        pack_d(0, 0)
-        pack_h(0, 1, 400)
-        quantize_d(0, 0)
-        pack_d(0, 1)
-        quantize_h(0, 1)
-        pack_d(0, 2)
-        quantize_d(0, 1)
-        quantize_d(0, 2)
-        for a in range(2):
-            multiply(0, 0, a, 0)
-        turn(1)
-        for a in range(2):
-            multiply(0, 0, a, 1)
-        pack_d(1, 0)
-        pack_h(0, 2, 400)
-        quantize_d(1, 0)
-        pack_d(1, 1)
-        quantize_h(0, 2)
-        pack_d(1, 2)
-        quantize_d(1, 1)
-        quantize_d(1, 2)
-        for a in range(2):
-            multiply(1, 0, a, 0)
-        turn(2)
-        for a in range(2):
-            multiply(0, 0, a, 2)
-        for c in range(1, 3):
-            for a in range(2):
-                multiply(1, 0, a, c)
-        pack_d(2, 0)
-        pack_d(2, 1)
-        pack_d(2, 2)
-        pack_h(1, 0, 256)
-        quantize_d(2, 0)
-        advect(0, 0, 0)
-        quantize_d(2, 1)
-        advect(0, 0, 1)
-        quantize_d(2, 2)
-        store_y(0, 0, 0, 2)
+        def mm_by_pass(pair, half, passes):
+            for c in passes:
+                for a in range(2):
+                    multiply(pair, half, a, c)
+
+        def pack_pair(pair):
+            for c in range(3):
+                pack_d(pair, c)
+
+        def interleave2(copy, packed, raw, lo, hi):
+            copy(out=packed[:].rearrange("p (c i) t -> p c t i", i=RUN), in_=raw[:, :, lo:hi].rearrange("p t (c i) -> p c t i", i=RUN))
+
+        def prepare(j):
+            turn(j)
+            pack_d(j, 0)
+            pack_h(0, j, 352)
+            pack_d(j, 1)
+            pack_d(j, 2)
+            quantize_d(j, 0)
+            quantize_h(0, j)
+            quantize_d(j, 1)
+
+        warm(18)
+        prepare(0)
+        warm(12)
+        prepare(1)
+        mm_by_pass(0, 0, [0])
+        prepare(2)
+        mm_by_pass(1, 0, [0])
+        mm_by_pass(0, 0, [1])
+        mm_by_pass(1, 0, [1])
+        mm_by_pass(0, 0, [2])
+        mm_by_pass(1, 0, [2])
+        pack_h(1, 0, 0)
         turn(3)
-        advect(1, 0, 0)
-        quantize_h(1, 0)
-        advect(1, 0, 1)
-        store_y(0, 0, 2, 4)
-        pack_d(3, 0)
-        pack_d(3, 1)
-        pack_d(3, 2)
-        pack_h(1, 1, 256)
-        quantize_d(3, 0)
-        quantize_d(3, 1)
-        quantize_d(3, 2)
+        finish(0, 0)
+        pack_pair(3)
+        finish(1, 0)
         mm(2, 0)
-        pack_h(1, 2, 192)
-        advect(2, 0, 0)
+        quantize_d(3, 0)
+        pack_h(1, 1, 192)
+        quantize_d(3, 1)
+        quantize_h(1, 0)
+        finish(2, 0)
+        pack_h(1, 2, 0)
         quantize_h(1, 1)
-        advect(2, 0, 1)
-        store_y(1, 0, 0, 2)
-        quantize_h(1, 2)
         mm(3, 0)
         turn(4)
         finish(3, 0)
-        ready_d(4)
-        pack_y(0, 0, 0)
-        mm(0, 1)
+        quantize_h(1, 2)
+        pack_pair(4)
+        mm_by_pass(0, 1, [0, 1, 2])
+        quantize_d(4, 0)
+        pack_y(0, 0, 128)
         finish(0, 1)
-        quantize_y(0, 0); store_codes(0, 0)
+        quantize_d(4, 1)
         pack_y(1, 0, 0)
         mm(1, 1)
         finish(1, 1)
+        quantize_y(0, 0); store_codes(0, 0)
         mm(2, 1)
-        advect(2, 1, 0)
-        quantize_y(1, 0)
-        advect(2, 1, 1)
-        store_codes(1, 0)
-        store_y(1, 1, 0, 2)
-        pack_y(0, 1, 0)
-        mm(3, 1)
         turn(5)
+        finish(2, 1)
+        pack_pair(5)
+        quantize_y(1, 0); store_codes(1, 0)
+        mm(3, 1)
+        quantize_d(5, 0)
+        pack_y(0, 1, 128)
         finish(3, 1)
-        quantize_y(0, 1); store_codes(0, 1)
-        ready_d(5)
+        quantize_d(5, 1)
         pack_y(1, 1, 0)
         mm(4, 0)
         finish(4, 0)
+        quantize_y(0, 1); store_codes(0, 1)
         mm(5, 0)
-        advect(5, 0, 0)
-        advect(5, 0, 1)
-        store_y(2, 0, 2, 4)
+        finish(5, 0)
         quantize_y(1, 1)
         store_codes(1, 1); store_scales(0, 2, [nc.sync])
         pack_y(2, 0, 0)
@@ -311,12 +303,14 @@ def tile_chebyshev_self_advection_g2_kernel(tc, D, h, p, out_0, out_1, out_2):
         mm(5, 1, 0, 256)
         advect_part(5, 1, 0, 0, 256)
         advect_part(5, 1, 1, 0, 256)
-        y_packed[2, 1, 0] = stage.tile([P, HALF, PACK], BF16, name="y_packed", align_bytes=64)
-        interleave(nc.scalar.copy, y_packed[2, 1, 0], y[2, 1, 0], 0, 256)
+        y_packed[2, 1, 0] = stage.tile([P, 256, PACK], BF16, name="y_packed", align_bytes=64)
+        interleave2(nc.scalar.copy, y_packed[2, 1, 0], y[2, 1, 0], 0, 256)
         mm(5, 1, 256, 512)
         advect_part(5, 1, 0, 256, 512)
         advect_part(5, 1, 1, 256, 512)
         store_y(2, 1, 2, 4)
         quantize_y(2, 0); store_codes(2, 0)
-        interleave(nc.vector.tensor_copy, y_packed[2, 1, 0], y[2, 1, 0], 256, 512)
-        quantize_y(2, 1); store_codes(2, 1); store_scales(2, 3, [nc.scalar, nc.sync])
+        y_packed[2, 1, 256] = stage.tile([P, 256, PACK], BF16, name="y_packed", align_bytes=64)
+        interleave2(nc.vector.tensor_copy, y_packed[2, 1, 256], y[2, 1, 0], 256, 512)
+        quantize_y(2, 1, 0, 256); store_codes(2, 1, 0, 256)
+        quantize_y(2, 1, 256, 512); store_codes(2, 1, 256, 512); store_scales(2, 3, [nc.scalar, nc.sync])

@@ -16,11 +16,23 @@ MULT = mybir.AluOpType.mult
 ADD = mybir.AluOpType.add
 
 P = 128
-PACK = 4
-GROUP = P * PACK
+SLOTS = 4
+GROUP = P * SLOTS
 GROUPS = POINTS // GROUP
-HALF = 512
+HALF = FIELDS // 2
+QUARTER = HALF // 2
 RUN = 4
+SCALE_ROWS = 4
+TURN_BANKS = GROUPS
+PRODUCT_BANKS = 8 - TURN_BANKS
+
+VECTOR_SHARE_FIRST_HALF = 384
+VECTOR_SHARE_SECOND_HALF = 256
+VECTOR_SHARE_LAST_PIECE = 192
+
+WARM_BEFORE_FIRST_PAIR = 16
+WARM_BEFORE_SECOND_PAIR = 8
+WARM_BEFORE_THIRD_PAIR = 4
 
 
 def tile_chebyshev_self_advection_g2_kernel(tc, D, h, p, out_0, out_1, out_2):
@@ -33,38 +45,33 @@ def tile_chebyshev_self_advection_g2_kernel(tc, D, h, p, out_0, out_1, out_2):
 
         h_raw, h_packed, h_codes, h_scales = {}, {}, {}, {}
         d_raw, d_bank, d_packed, d_codes, d_scales = {}, {}, {}, {}, {}
-        acc, y, y_packed, y_codes, y_scales = {}, {}, {}, {}, {}
-        words_out = out_1.rearrange("g p m t -> g p (m t)").bitcast(I32)
+        slope, y, y_packed, y_codes, y_scales = {}, {}, {}, {}, {}
+        codes_out = out_1.rearrange("g p m t -> g p (m t)").bitcast(I32)
         scales_out = out_2.bitcast(I32)
 
         def load_h(half, g):
-            h_raw[half, g] = keep.tile([P, PACK, HALF], BF16, name="h_raw_%d_%d" % (half, g), align_bytes=64)
+            h_raw[half, g] = keep.tile([P, SLOTS, HALF], BF16, name="h_raw_%d_%d" % (half, g), align_bytes=64)
             rows = h[GROUP * g : GROUP * (g + 1), HALF * half : HALF * (half + 1)]
-            nc.sync.dma_start(out=h_raw[half, g][:], in_=rows.rearrange("(p t) n -> p t n", t=PACK))
+            nc.sync.dma_start(out=h_raw[half, g][:], in_=rows.rearrange("(p t) n -> p t n", t=SLOTS))
 
         def load_d(pair):
             g, q = divmod(pair, 2)
             d_raw[pair] = keep.tile([P, 2, POINTS], BF16, name="d_raw_%d" % pair, align_bytes=64)
-            rows = D[GROUP * g : GROUP * (g + 1), :].rearrange("(m t) k -> m t k", t=PACK)
+            rows = D[GROUP * g : GROUP * (g + 1), :].rearrange("(m t) k -> m t k", t=SLOTS)
             nc.sync.dma_start(out=d_raw[pair][:], in_=rows[:, 2 * q : 2 * q + 2, :])
 
-        def interleave(copy, packed, raw, lo, hi):
-            copy(
-                out=packed[:, lo:hi, :].rearrange("p (c i) t -> p c t i", i=RUN),
-                in_=raw[:, :, lo:hi].rearrange("p t (c i) -> p c t i", i=RUN),
-            )
+        def interleave(packed, source, vector_share):
+            width = source.shape[2]
+            for copy, lo, hi in ((nc.vector.tensor_copy, 0, vector_share), (nc.scalar.copy, vector_share, width)):
+                if hi > lo:
+                    copy(
+                        out=packed[:, lo:hi, :].rearrange("p (c i) t -> p c t i", i=RUN),
+                        in_=source[:, :, lo:hi].rearrange("p t (c i) -> p c t i", i=RUN),
+                    )
 
-        def pack_h_part(copy, half, g, lo, hi):
-            if lo == 0:
-                h_packed[half, g] = stage.tile([P, HALF, PACK], BF16, name="h_packed", align_bytes=64)
-            interleave(copy, h_packed[half, g], h_raw[half, g], lo, hi)
-
-        def pack_h(half, g, split):
-            h_packed[half, g] = stage.tile([P, HALF, PACK], BF16, name="h_packed", align_bytes=64)
-            if split > 0:
-                interleave(nc.vector.tensor_copy, h_packed[half, g], h_raw[half, g], 0, split)
-            if split < HALF:
-                interleave(nc.scalar.copy, h_packed[half, g], h_raw[half, g], split, HALF)
+        def pack_h(half, g, vector_share):
+            h_packed[half, g] = stage.tile([P, HALF, SLOTS], BF16, name="h_packed", align_bytes=64)
+            interleave(h_packed[half, g], h_raw[half, g][:], vector_share)
 
         def quantize_h(half, g):
             h_codes[half, g] = keep.tile([P, HALF], U32, name="h_codes_%d_%d" % (half, g), align_bytes=64)
@@ -75,23 +82,30 @@ def tile_chebyshev_self_advection_g2_kernel(tc, D, h, p, out_0, out_1, out_2):
                 in_=h_packed[half, g][:].rearrange("p n t -> p (n t)"),
             )
 
-        def turn_d(pair, c):
+        def turn_d(pair):
             words = d_raw[pair][:].rearrange("p a k -> p (a k)").bitcast(F32)
-            bank = psum.tile([P, 2, 2, P], F32, name="d_bank", bufs=3)
-            for a in range(2):
-                for u in range(2):
-                    base = a * POINTS // 2 + c * GROUP // 2
-                    nc.tensor.transpose(bank[:, a, u, :], words[:, base + u : base + GROUP // 2 : 2], identity[:])
-            d_bank[pair, c] = bank
+            for c in range(GROUPS):
+                bank = psum.tile([P, 2, 2, P], F32, name="d_bank", bufs=TURN_BANKS)
+                for a in range(2):
+                    first_word = (a * POINTS + c * GROUP) // 2
+                    for u in range(2):
+                        nc.tensor.transpose(
+                            bank[:, a, u, :], words[:, first_word + u : first_word + GROUP // 2 : 2], identity[:]
+                        )
+                d_bank[pair, c] = bank
 
-        def pack_d(pair, c):
-            if c < 2:
-                d_packed[pair, c] = stage.tile([P, 2 * GROUP * (c + 1)], BF16, name="d_packed_%d" % c, bufs=2, align_bytes=64)
-            part = d_packed[pair, min(c, 1)][:, 2 * GROUP * (c // 2) : 2 * GROUP * (c // 2 + 1)]
-            nc.scalar.copy(
-                out=part.bitcast(F32).rearrange("p (a m u) -> p a m u", a=2, u=2),
-                in_=d_bank[pair, c][:].rearrange("p a u m -> p a m u"),
-            )
+        def pack_d(pair, passes):
+            for c in passes:
+                part = min(c, 1)
+                if c == part:
+                    d_packed[pair, part] = stage.tile(
+                        [P, 2 * GROUP * (part + 1)], BF16, name="d_packed_%d" % part, bufs=2, align_bytes=64
+                    )
+                columns = d_packed[pair, part][:, 2 * GROUP * (c - part) : 2 * GROUP * (c - part + 1)]
+                nc.scalar.copy(
+                    out=columns.bitcast(F32).rearrange("p (a m u) -> p a m u", a=2, u=2),
+                    in_=d_bank[pair, c][:].rearrange("p a u m -> p a m u"),
+                )
 
         def quantize_d(pair, part):
             width = 2 * P * (part + 1)
@@ -102,215 +116,195 @@ def tile_chebyshev_self_advection_g2_kernel(tc, D, h, p, out_0, out_1, out_2):
                 d_codes[pair, part + j] = codes[:, 2 * P * j : 2 * P * (j + 1)]
                 d_scales[pair, part + j] = scales[:, 2 * P * j : 2 * P * (j + 1)]
 
-        def multiply(pair, half, a, c, lo=0, hi=HALF):
+        def one_pass(pair, half, a, c, lo, hi):
             if c == 0:
-                acc[pair, half, a, lo] = psum.tile([P, hi - lo], F32, name="acc", bufs=5)
-            cols = slice(a * P, (a + 1) * P)
+                slope[pair, half, a, lo] = psum.tile([P, hi - lo], F32, name="product", bufs=PRODUCT_BANKS)
+            rows = slice(a * P, (a + 1) * P)
             nc.tensor.matmul_mx(
-                out=acc[pair, half, a, lo][:],
-                lhsT=d_codes[pair, c][:, cols].bitcast(FP8X4),
-                lhsT_scale=d_scales[pair, c][:, cols],
+                out=slope[pair, half, a, lo][:],
+                lhsT=d_codes[pair, c][:, rows].bitcast(FP8X4),
+                lhsT_scale=d_scales[pair, c][:, rows],
                 rhs=h_codes[half, c][:, lo:hi].bitcast(FP8X4),
                 rhs_scale=h_scales[half, c][:, lo:hi],
                 start=(c == 0),
                 stop=(c == GROUPS - 1),
             )
 
-        def advect(pair, half, a, lo=0, hi=HALF):
+        def multiply(pair, half, lo=0, hi=HALF):
+            for a in range(2):
+                for c in range(GROUPS):
+                    one_pass(pair, half, a, c, lo, hi)
+
+        def multiply_pass(pair, half, c):
+            for a in range(2):
+                one_pass(pair, half, a, c, 0, HALF)
+
+        def advect(pair, half, lo=0, hi=HALF):
             g, q = divmod(pair, 2)
-            t = 2 * q + a
-            if t == 0:
-                y[g, half, lo] = stage.tile([P, PACK, hi - lo], F32, name="y", bufs=5, align_bytes=64)
-            nc.vector.scalar_tensor_tensor(
-                out=y[g, half, lo][:, t, :],
-                in0=h_raw[half, g][:, t, lo:hi],
-                scalar=minus_p[:, g, t : t + 1],
-                in1=acc[pair, half, a, lo][:],
-                op0=MULT,
-                op1=MULT,
-            )
-
-        def advect_part(pair, half, a, lo, hi):
-            g, q = divmod(pair, 2)
-            t = 2 * q + a
-            nc.vector.scalar_tensor_tensor(
-                out=y[g, half, 0][:, t, lo:hi],
-                in0=h_raw[half, g][:, t, lo:hi],
-                scalar=minus_p[:, g, t : t + 1],
-                in1=acc[pair, half, a, lo][:],
-                op0=MULT,
-                op1=MULT,
-            )
-
-        def store_y(g, half, t0, t1, lo=0, hi=HALF):
-            rows = out_0[GROUP * g : GROUP * (g + 1), HALF * half + lo : HALF * half + hi]
-            nc.sync.dma_start(
-                out=rows.rearrange("(p t) n -> p t n", t=PACK)[:, t0:t1, :], in_=y[g, half, lo][:, t0:t1, :]
-            )
-
-        def pack_y(g, half, split, lo=0, hi=HALF):
-            y_packed[g, half, lo] = stage.tile([P, hi - lo, PACK], BF16, name="y_packed", align_bytes=64)
-            if split > 0:
-                interleave(nc.vector.tensor_copy, y_packed[g, half, lo], y[g, half, lo], 0, split)
-            if split < hi - lo:
-                interleave(nc.scalar.copy, y_packed[g, half, lo], y[g, half, lo], split, hi - lo)
-
-        def quantize_y(g, half, lo=0, hi=HALF):
-            y_codes[g, half, lo] = stage.tile([P, hi - lo], U32, name="y_codes", align_bytes=64)
-            if half == 0 and lo == 0 and g != 1:
-                y_scales[g // 2] = keep.tile([P, FIELDS], U8, name="y_scales_%d" % (g // 2), align_bytes=64)
-            nc.vector.quantize_mx(
-                out=y_codes[g, half, lo][:].bitcast(FP8X4),
-                scales=y_scales[g // 2][4 * (g % 2) :, HALF * half + lo : HALF * half + hi],
-                in_=y_packed[g, half, lo][:].rearrange("p n t -> p (n t)"),
-            )
-
-        def store_codes(g, half, lo=0, hi=HALF):
-            nc.sync.dma_start(
-                out=words_out[g, :, HALF * half + lo : HALF * half + hi], in_=y_codes[g, half, lo][:].bitcast(I32)
-            )
-
-        def store_scales(g0, g1, queues):
-            for quad in range(4):
-                queues[quad % len(queues)].dma_start(
-                    out=scales_out[g0:g1, 4 * quad : 4 * quad + 4, :],
-                    in_=y_scales[g0 // 2][32 * quad : 32 * quad + 4 * (g1 - g0), :].bitcast(I32),
+            if q == 0:
+                y[g, half] = stage.tile([P, SLOTS, HALF], F32, name="y", bufs=5, align_bytes=64)
+            for a in range(2):
+                t = 2 * q + a
+                nc.vector.scalar_tensor_tensor(
+                    out=y[g, half][:, t, lo:hi],
+                    in0=h_raw[half, g][:, t, lo:hi],
+                    scalar=minus_p[:, g, t : t + 1],
+                    in1=slope[pair, half, a, lo][:],
+                    op0=MULT,
+                    op1=MULT,
                 )
 
-        p_raw = keep.tile([P, GROUPS, PACK], BF16, name="p_raw")
-        minus_p = keep.tile([P, GROUPS, PACK], F32, name="minus_p")
-        identity = keep.tile([P, P], F32, name="identity")
-
-        load_d(0); load_h(0, 0); load_d(1); load_h(0, 1); load_d(2); load_h(0, 2); load_h(1, 0); load_d(3)
-        load_h(1, 1); load_h(1, 2); load_d(4); load_d(5)
-        nc.gpsimd.dma_start(out=p_raw[:], in_=p.rearrange("(g p t) -> p g t", p=P, t=PACK))
-        make_identity(nc, identity[:])
-        nc.gpsimd.tensor_scalar(out=minus_p[:], in0=p_raw[:], scalar1=-1.0, scalar2=0.0, op0=MULT, op1=ADD)
-
-        def mm(pair, half, lo=0, hi=HALF):
-            for a in range(2):
-                for c in range(3):
-                    multiply(pair, half, a, c, lo, hi)
-
-        def turn(pair):
-            for c in range(3):
-                turn_d(pair, c)
-
-        def ready_d(pair):
-            for c in range(3):
-                pack_d(pair, c)
-                quantize_d(pair, c)
+        def store_y(pair, half):
+            g, q = divmod(pair, 2)
+            rows = out_0[GROUP * g : GROUP * (g + 1), HALF * half : HALF * (half + 1)]
+            nc.sync.dma_start(
+                out=rows.rearrange("(p t) n -> p t n", t=SLOTS)[:, 2 * q : 2 * q + 2, :],
+                in_=y[g, half][:, 2 * q : 2 * q + 2, :],
+            )
 
         def finish(pair, half):
-            g, q = divmod(pair, 2)
-            advect(pair, half, 0)
-            advect(pair, half, 1)
-            store_y(g, half, 2 * q, 2 * q + 2)
+            advect(pair, half)
+            store_y(pair, half)
 
-        warm_in = keep.tile([P, GROUP], BF16, name="warm_in", align_bytes=64)
-        warm_codes = keep.tile([P, P], U32, name="warm_codes", align_bytes=64)
-        warm_scales = keep.tile([P, P], U8, name="warm_scales", align_bytes=64)
-        nc.vector.memset(warm_in[:], 1.0)
-        nc.vector.quantize_mx(out=warm_codes[:].bitcast(FP8X4), scales=warm_scales[:], in_=warm_in[:])
+        def pack_y(g, half, lo=0, hi=HALF, vector_share=0):
+            y_packed[g, half, lo] = stage.tile([P, hi - lo, SLOTS], BF16, name="y_packed", align_bytes=64)
+            interleave(y_packed[g, half, lo], y[g, half][:, :, lo:hi], vector_share)
 
-        def warm(n):
-            bank = psum.tile([P, P], F32, name="acc", bufs=5)
-            for i in range(n):
-                nc.tensor.matmul_mx(out=bank[:], lhsT=warm_codes[:].bitcast(FP8X4), lhsT_scale=warm_scales[:],
-                                    rhs=warm_codes[:].bitcast(FP8X4), rhs_scale=warm_scales[:], start=True, stop=True)
+        def emit_codes(g, half, lo=0, hi=HALF):
+            columns = slice(HALF * half + lo, HALF * half + hi)
+            codes = stage.tile([P, hi - lo], U32, name="y_codes", align_bytes=64)
+            if half == 0 and g < 2:
+                y_scales[g] = keep.tile([P, FIELDS], U8, name="y_scales_%d" % g, align_bytes=64)
+            nc.vector.quantize_mx(
+                out=codes[:].bitcast(FP8X4),
+                scales=y_scales[min(g, 1)][SCALE_ROWS * (g // 2) :, columns],
+                in_=y_packed[g, half, lo][:].rearrange("p n t -> p (n t)"),
+            )
+            nc.sync.dma_start(out=codes_out[g, :, columns], in_=codes[:].bitcast(I32))
 
-        def mm_by_pass(pair, half, passes):
-            for c in passes:
-                for a in range(2):
-                    multiply(pair, half, a, c)
+        def store_scales(first_group, groups, queues):
+            for quad in range(4):
+                queues[quad % len(queues)].dma_start(
+                    out=scales_out[first_group : first_group + groups, SCALE_ROWS * quad : SCALE_ROWS * (quad + 1), :],
+                    in_=y_scales[first_group][32 * quad : 32 * quad + SCALE_ROWS * groups, :].bitcast(I32),
+                )
 
-        def pack_pair(pair):
-            for c in range(3):
-                pack_d(pair, c)
-
-        def interleave2(copy, packed, raw, lo, hi):
-            copy(out=packed[:].rearrange("p (c i) t -> p c t i", i=RUN), in_=raw[:, :, lo:hi].rearrange("p t (c i) -> p c t i", i=RUN))
+        def warm(passes):
+            bank = psum.tile([P, P], F32, name="product", bufs=PRODUCT_BANKS)
+            for i in range(passes):
+                nc.tensor.matmul_mx(
+                    out=bank[:],
+                    lhsT=warm_codes[:].bitcast(FP8X4),
+                    lhsT_scale=warm_scales[:],
+                    rhs=warm_codes[:].bitcast(FP8X4),
+                    rhs_scale=warm_scales[:],
+                    start=True,
+                    stop=True,
+                )
 
         def prepare(j):
-            turn(j)
-            pack_d(j, 0)
-            pack_h(0, j, 352)
-            pack_d(j, 1)
-            pack_d(j, 2)
+            turn_d(j)
+            pack_d(j, [0])
+            pack_h(0, j, VECTOR_SHARE_FIRST_HALF)
+            pack_d(j, [1, 2])
             quantize_d(j, 0)
             quantize_h(0, j)
             quantize_d(j, 1)
 
-        warm(18)
+        p_raw = keep.tile([P, GROUPS, SLOTS], BF16, name="p_raw")
+        minus_p = keep.tile([P, GROUPS, SLOTS], F32, name="minus_p")
+        identity = keep.tile([P, P], F32, name="identity")
+        for j in range(GROUPS):
+            load_d(j)
+            load_h(0, j)
+        load_h(1, 0)
+        load_d(3)
+        load_h(1, 1)
+        load_h(1, 2)
+        load_d(4)
+        load_d(5)
+        nc.gpsimd.dma_start(out=p_raw[:], in_=p.rearrange("(g p t) -> p g t", p=P, t=SLOTS))
+        make_identity(nc, identity[:])
+        nc.gpsimd.tensor_scalar(out=minus_p[:], in0=p_raw[:], scalar1=-1.0, scalar2=0.0, op0=MULT, op1=ADD)
+
+        warm_ones = keep.tile([P, GROUP], BF16, name="warm_ones", align_bytes=64)
+        warm_codes = keep.tile([P, P], U32, name="warm_codes", align_bytes=64)
+        warm_scales = keep.tile([P, P], U8, name="warm_scales", align_bytes=64)
+        nc.vector.memset(warm_ones[:], 1.0)
+        nc.vector.quantize_mx(out=warm_codes[:].bitcast(FP8X4), scales=warm_scales[:], in_=warm_ones[:])
+
+        warm(WARM_BEFORE_FIRST_PAIR)
         prepare(0)
-        warm(12)
+        warm(WARM_BEFORE_SECOND_PAIR)
         prepare(1)
-        mm_by_pass(0, 0, [0])
+        multiply_pass(0, 0, 0)
+        warm(WARM_BEFORE_THIRD_PAIR)
         prepare(2)
-        mm_by_pass(1, 0, [0])
-        mm_by_pass(0, 0, [1])
-        mm_by_pass(1, 0, [1])
-        mm_by_pass(0, 0, [2])
-        mm_by_pass(1, 0, [2])
+        multiply_pass(1, 0, 0)
+        for c in range(1, GROUPS):
+            for pair in range(2):
+                multiply_pass(pair, 0, c)
+
         pack_h(1, 0, 0)
-        turn(3)
+        turn_d(3)
         finish(0, 0)
-        pack_pair(3)
+        pack_d(3, range(GROUPS))
         finish(1, 0)
-        mm(2, 0)
+        multiply(2, 0)
         quantize_d(3, 0)
-        pack_h(1, 1, 192)
+        pack_h(1, 1, VECTOR_SHARE_SECOND_HALF)
         quantize_d(3, 1)
         quantize_h(1, 0)
         finish(2, 0)
         pack_h(1, 2, 0)
         quantize_h(1, 1)
-        mm(3, 0)
-        turn(4)
+        multiply(3, 0)
+        turn_d(4)
         finish(3, 0)
         quantize_h(1, 2)
-        pack_pair(4)
-        mm_by_pass(0, 1, [0, 1, 2])
+        pack_d(4, range(GROUPS))
+
+        for c in range(GROUPS):
+            multiply_pass(0, 1, c)
         quantize_d(4, 0)
-        pack_y(0, 0, 128)
-        finish(0, 1)
+        pack_y(0, 0)
         quantize_d(4, 1)
-        pack_y(1, 0, 0)
-        mm(1, 1)
+        finish(0, 1)
+        pack_y(1, 0)
+        multiply(1, 1)
         finish(1, 1)
-        quantize_y(0, 0); store_codes(0, 0)
-        mm(2, 1)
-        turn(5)
+        emit_codes(0, 0)
+        multiply(2, 1)
+        turn_d(5)
         finish(2, 1)
-        pack_pair(5)
-        quantize_y(1, 0); store_codes(1, 0)
-        mm(3, 1)
+        pack_d(5, range(GROUPS))
+        emit_codes(1, 0)
+        multiply(3, 1)
         quantize_d(5, 0)
-        pack_y(0, 1, 128)
-        finish(3, 1)
+        pack_y(0, 1)
         quantize_d(5, 1)
-        pack_y(1, 1, 0)
-        mm(4, 0)
+        finish(3, 1)
+        pack_y(1, 1)
+
+        multiply(4, 0)
         finish(4, 0)
-        quantize_y(0, 1); store_codes(0, 1)
-        mm(5, 0)
+        emit_codes(0, 1)
+        store_scales(0, 1, [nc.sync])
+        multiply(5, 0)
         finish(5, 0)
-        quantize_y(1, 1)
-        store_codes(1, 1); store_scales(0, 2, [nc.sync])
-        pack_y(2, 0, 0)
-        mm(4, 1)
+        emit_codes(1, 1)
+        pack_y(2, 0)
+
+        multiply(4, 1)
         finish(4, 1)
-        mm(5, 1, 0, 256)
-        advect_part(5, 1, 0, 0, 256)
-        advect_part(5, 1, 1, 0, 256)
-        y_packed[2, 1, 0] = stage.tile([P, 256, PACK], BF16, name="y_packed", align_bytes=64)
-        interleave2(nc.scalar.copy, y_packed[2, 1, 0], y[2, 1, 0], 0, 256)
-        mm(5, 1, 256, 512)
-        advect_part(5, 1, 0, 256, 512)
-        advect_part(5, 1, 1, 256, 512)
-        store_y(2, 1, 2, 4)
-        quantize_y(2, 0); store_codes(2, 0)
-        y_packed[2, 1, 256] = stage.tile([P, 256, PACK], BF16, name="y_packed", align_bytes=64)
-        interleave2(nc.vector.tensor_copy, y_packed[2, 1, 256], y[2, 1, 0], 256, 512)
-        quantize_y(2, 1, 0, 256); store_codes(2, 1, 0, 256)
-        quantize_y(2, 1, 256, 512); store_codes(2, 1, 256, 512); store_scales(2, 3, [nc.scalar, nc.sync])
+        multiply(5, 1, 0, QUARTER)
+        advect(5, 1, 0, QUARTER)
+        pack_y(2, 1, 0, QUARTER)
+        multiply(5, 1, QUARTER, HALF)
+        advect(5, 1, QUARTER, HALF)
+        store_y(5, 1)
+        emit_codes(2, 0)
+        pack_y(2, 1, QUARTER, HALF, VECTOR_SHARE_LAST_PIECE)
+        emit_codes(2, 1, 0, QUARTER)
+        emit_codes(2, 1, QUARTER, HALF)
+        store_scales(1, 2, [nc.scalar, nc.sync])

from contextlib import ExitStack

import concourse.mybir as mybir
from concourse.masks import make_identity

POINTS, FIELDS = 1536, 1024
FLOPS = 2 * POINTS * POINTS * FIELDS

F32 = mybir.dt.float32
BF16 = mybir.dt.bfloat16
U32 = mybir.dt.uint32
I32 = mybir.dt.int32
U8 = mybir.dt.uint8
FP8X4 = mybir.dt.float8_e4m3fn_x4
MULT = mybir.AluOpType.mult
ADD = mybir.AluOpType.add

P = 128
SLOTS = 4
GROUP = P * SLOTS
GROUPS = POINTS // GROUP
HALF = FIELDS // 2
QUARTER = HALF // 2
RUN = 4
SCALE_ROWS = 4
TURN_BANKS = GROUPS
PRODUCT_BANKS = 8 - TURN_BANKS

VECTOR_SHARE_FIRST_HALF = 384
VECTOR_SHARE_SECOND_HALF = 256
VECTOR_SHARE_LAST_PIECE = 192

WARM_BEFORE_FIRST_PAIR = 16
WARM_BEFORE_SECOND_PAIR = 8
WARM_BEFORE_THIRD_PAIR = 4


def tile_chebyshev_self_advection_g2_kernel(tc, D, h, p, out_0, out_1, out_2):
    nc = tc.nc
    with ExitStack() as ctx:
        keep = ctx.enter_context(tc.tile_pool(name="keep", bufs=1))
        stage = ctx.enter_context(tc.tile_pool(name="stage", bufs=3))
        psum = ctx.enter_context(tc.psum_pool(name="psum", bufs=1))
        ctx.enter_context(tc.manual_schedule())

        h_raw, h_packed, h_codes, h_scales = {}, {}, {}, {}
        d_raw, d_bank, d_packed, d_codes, d_scales = {}, {}, {}, {}, {}
        slope, y, y_packed, y_codes, y_scales = {}, {}, {}, {}, {}
        codes_out = out_1.rearrange("g p m t -> g p (m t)").bitcast(I32)
        scales_out = out_2.bitcast(I32)

        def load_h(half, g):
            h_raw[half, g] = keep.tile([P, SLOTS, HALF], BF16, name="h_raw_%d_%d" % (half, g), align_bytes=64)
            rows = h[GROUP * g : GROUP * (g + 1), HALF * half : HALF * (half + 1)]
            nc.sync.dma_start(out=h_raw[half, g][:], in_=rows.rearrange("(p t) n -> p t n", t=SLOTS))

        def load_d(pair):
            g, q = divmod(pair, 2)
            d_raw[pair] = keep.tile([P, 2, POINTS], BF16, name="d_raw_%d" % pair, align_bytes=64)
            rows = D[GROUP * g : GROUP * (g + 1), :].rearrange("(m t) k -> m t k", t=SLOTS)
            nc.sync.dma_start(out=d_raw[pair][:], in_=rows[:, 2 * q : 2 * q + 2, :])

        def interleave(packed, source, vector_share):
            width = source.shape[2]
            for copy, lo, hi in ((nc.vector.tensor_copy, 0, vector_share), (nc.scalar.copy, vector_share, width)):
                if hi > lo:
                    copy(
                        out=packed[:, lo:hi, :].rearrange("p (c i) t -> p c t i", i=RUN),
                        in_=source[:, :, lo:hi].rearrange("p t (c i) -> p c t i", i=RUN),
                    )

        def pack_h(half, g, vector_share):
            h_packed[half, g] = stage.tile([P, HALF, SLOTS], BF16, name="h_packed", align_bytes=64)
            interleave(h_packed[half, g], h_raw[half, g][:], vector_share)

        def quantize_h(half, g):
            h_codes[half, g] = keep.tile([P, HALF], U32, name="h_codes_%d_%d" % (half, g), align_bytes=64)
            h_scales[half, g] = keep.tile([P, HALF], U8, name="h_scales_%d_%d" % (half, g), align_bytes=64)
            nc.vector.quantize_mx(
                out=h_codes[half, g][:].bitcast(FP8X4),
                scales=h_scales[half, g][:],
                in_=h_packed[half, g][:].rearrange("p n t -> p (n t)"),
            )

        def turn_d(pair):
            words = d_raw[pair][:].rearrange("p a k -> p (a k)").bitcast(F32)
            for c in range(GROUPS):
                bank = psum.tile([P, 2, 2, P], F32, name="d_bank", bufs=TURN_BANKS)
                for a in range(2):
                    first_word = (a * POINTS + c * GROUP) // 2
                    for u in range(2):
                        nc.tensor.transpose(
                            bank[:, a, u, :], words[:, first_word + u : first_word + GROUP // 2 : 2], identity[:]
                        )
                d_bank[pair, c] = bank

        def pack_d(pair, passes):
            for c in passes:
                part = min(c, 1)
                if c == part:
                    d_packed[pair, part] = stage.tile(
                        [P, 2 * GROUP * (part + 1)], BF16, name="d_packed_%d" % part, bufs=2, align_bytes=64
                    )
                columns = d_packed[pair, part][:, 2 * GROUP * (c - part) : 2 * GROUP * (c - part + 1)]
                nc.scalar.copy(
                    out=columns.bitcast(F32).rearrange("p (a m u) -> p a m u", a=2, u=2),
                    in_=d_bank[pair, c][:].rearrange("p a u m -> p a m u"),
                )

        def quantize_d(pair, part):
            width = 2 * P * (part + 1)
            codes = keep.tile([P, width], U32, name="d_codes_%d_%d" % (pair, part), align_bytes=64)
            scales = keep.tile([P, width], U8, name="d_scales_%d_%d" % (pair, part), align_bytes=64)
            nc.vector.quantize_mx(out=codes[:].bitcast(FP8X4), scales=scales[:], in_=d_packed[pair, part][:])
            for j in range(part + 1):
                d_codes[pair, part + j] = codes[:, 2 * P * j : 2 * P * (j + 1)]
                d_scales[pair, part + j] = scales[:, 2 * P * j : 2 * P * (j + 1)]

        def one_pass(pair, half, a, c, lo, hi):
            if c == 0:
                slope[pair, half, a, lo] = psum.tile([P, hi - lo], F32, name="product", bufs=PRODUCT_BANKS)
            rows = slice(a * P, (a + 1) * P)
            nc.tensor.matmul_mx(
                out=slope[pair, half, a, lo][:],
                lhsT=d_codes[pair, c][:, rows].bitcast(FP8X4),
                lhsT_scale=d_scales[pair, c][:, rows],
                rhs=h_codes[half, c][:, lo:hi].bitcast(FP8X4),
                rhs_scale=h_scales[half, c][:, lo:hi],
                start=(c == 0),
                stop=(c == GROUPS - 1),
            )

        def multiply(pair, half, lo=0, hi=HALF):
            for a in range(2):
                for c in range(GROUPS):
                    one_pass(pair, half, a, c, lo, hi)

        def multiply_pass(pair, half, c):
            for a in range(2):
                one_pass(pair, half, a, c, 0, HALF)

        def advect(pair, half, lo=0, hi=HALF):
            g, q = divmod(pair, 2)
            if q == 0:
                y[g, half] = stage.tile([P, SLOTS, HALF], F32, name="y", bufs=5, align_bytes=64)
            for a in range(2):
                t = 2 * q + a
                nc.vector.scalar_tensor_tensor(
                    out=y[g, half][:, t, lo:hi],
                    in0=h_raw[half, g][:, t, lo:hi],
                    scalar=minus_p[:, g, t : t + 1],
                    in1=slope[pair, half, a, lo][:],
                    op0=MULT,
                    op1=MULT,
                )

        def store_y(pair, half):
            g, q = divmod(pair, 2)
            rows = out_0[GROUP * g : GROUP * (g + 1), HALF * half : HALF * (half + 1)]
            nc.sync.dma_start(
                out=rows.rearrange("(p t) n -> p t n", t=SLOTS)[:, 2 * q : 2 * q + 2, :],
                in_=y[g, half][:, 2 * q : 2 * q + 2, :],
            )

        def finish(pair, half):
            advect(pair, half)
            store_y(pair, half)

        def pack_y(g, half, lo=0, hi=HALF, vector_share=0):
            y_packed[g, half, lo] = stage.tile([P, hi - lo, SLOTS], BF16, name="y_packed", align_bytes=64)
            interleave(y_packed[g, half, lo], y[g, half][:, :, lo:hi], vector_share)

        def emit_codes(g, half, lo=0, hi=HALF):
            columns = slice(HALF * half + lo, HALF * half + hi)
            codes = stage.tile([P, hi - lo], U32, name="y_codes", align_bytes=64)
            if half == 0 and g < 2:
                y_scales[g] = keep.tile([P, FIELDS], U8, name="y_scales_%d" % g, align_bytes=64)
            nc.vector.quantize_mx(
                out=codes[:].bitcast(FP8X4),
                scales=y_scales[min(g, 1)][SCALE_ROWS * (g // 2) :, columns],
                in_=y_packed[g, half, lo][:].rearrange("p n t -> p (n t)"),
            )
            nc.sync.dma_start(out=codes_out[g, :, columns], in_=codes[:].bitcast(I32))

        def store_scales(first_group, groups, queues):
            for quad in range(4):
                queues[quad % len(queues)].dma_start(
                    out=scales_out[first_group : first_group + groups, SCALE_ROWS * quad : SCALE_ROWS * (quad + 1), :],
                    in_=y_scales[first_group][32 * quad : 32 * quad + SCALE_ROWS * groups, :].bitcast(I32),
                )

        def warm(passes):
            bank = psum.tile([P, P], F32, name="product", bufs=PRODUCT_BANKS)
            for i in range(passes):
                nc.tensor.matmul_mx(
                    out=bank[:],
                    lhsT=warm_codes[:].bitcast(FP8X4),
                    lhsT_scale=warm_scales[:],
                    rhs=warm_codes[:].bitcast(FP8X4),
                    rhs_scale=warm_scales[:],
                    start=True,
                    stop=True,
                )

        def prepare(j):
            turn_d(j)
            pack_d(j, [0])
            pack_h(0, j, VECTOR_SHARE_FIRST_HALF)
            pack_d(j, [1, 2])
            quantize_d(j, 0)
            quantize_h(0, j)
            quantize_d(j, 1)

        p_raw = keep.tile([P, GROUPS, SLOTS], BF16, name="p_raw")
        minus_p = keep.tile([P, GROUPS, SLOTS], F32, name="minus_p")
        identity = keep.tile([P, P], F32, name="identity")
        for j in range(GROUPS):
            load_d(j)
            load_h(0, j)
        load_h(1, 0)
        load_d(3)
        load_h(1, 1)
        load_h(1, 2)
        load_d(4)
        load_d(5)
        nc.gpsimd.dma_start(out=p_raw[:], in_=p.rearrange("(g p t) -> p g t", p=P, t=SLOTS))
        make_identity(nc, identity[:])
        nc.gpsimd.tensor_scalar(out=minus_p[:], in0=p_raw[:], scalar1=-1.0, scalar2=0.0, op0=MULT, op1=ADD)

        warm_ones = keep.tile([P, GROUP], BF16, name="warm_ones", align_bytes=64)
        warm_codes = keep.tile([P, P], U32, name="warm_codes", align_bytes=64)
        warm_scales = keep.tile([P, P], U8, name="warm_scales", align_bytes=64)
        nc.vector.memset(warm_ones[:], 1.0)
        nc.vector.quantize_mx(out=warm_codes[:].bitcast(FP8X4), scales=warm_scales[:], in_=warm_ones[:])

        warm(WARM_BEFORE_FIRST_PAIR)
        prepare(0)
        warm(WARM_BEFORE_SECOND_PAIR)
        prepare(1)
        multiply_pass(0, 0, 0)
        warm(WARM_BEFORE_THIRD_PAIR)
        prepare(2)
        multiply_pass(1, 0, 0)
        for c in range(1, GROUPS):
            for pair in range(2):
                multiply_pass(pair, 0, c)

        pack_h(1, 0, 0)
        turn_d(3)
        finish(0, 0)
        pack_d(3, range(GROUPS))
        finish(1, 0)
        multiply(2, 0)
        quantize_d(3, 0)
        pack_h(1, 1, VECTOR_SHARE_SECOND_HALF)
        quantize_d(3, 1)
        quantize_h(1, 0)
        finish(2, 0)
        pack_h(1, 2, 0)
        quantize_h(1, 1)
        multiply(3, 0)
        turn_d(4)
        finish(3, 0)
        quantize_h(1, 2)
        pack_d(4, range(GROUPS))

        for c in range(GROUPS):
            multiply_pass(0, 1, c)
        quantize_d(4, 0)
        pack_y(0, 0)
        quantize_d(4, 1)
        finish(0, 1)
        pack_y(1, 0)
        multiply(1, 1)
        finish(1, 1)
        emit_codes(0, 0)
        multiply(2, 1)
        turn_d(5)
        finish(2, 1)
        pack_d(5, range(GROUPS))
        emit_codes(1, 0)
        multiply(3, 1)
        quantize_d(5, 0)
        pack_y(0, 1)
        quantize_d(5, 1)
        finish(3, 1)
        pack_y(1, 1)

        multiply(4, 0)
        finish(4, 0)
        emit_codes(0, 1)
        store_scales(0, 1, [nc.sync])
        multiply(5, 0)
        finish(5, 0)
        emit_codes(1, 1)
        pack_y(2, 0)

        multiply(4, 1)
        finish(4, 1)
        multiply(5, 1, 0, QUARTER)
        advect(5, 1, 0, QUARTER)
        pack_y(2, 1, 0, QUARTER)
        multiply(5, 1, QUARTER, HALF)
        advect(5, 1, QUARTER, HALF)
        store_y(5, 1)
        emit_codes(2, 0)
        pack_y(2, 1, QUARTER, HALF, VECTOR_SHARE_LAST_PIECE)
        emit_codes(2, 1, 0, QUARTER)
        emit_codes(2, 1, QUARTER, HALF)
        store_scales(1, 2, [nc.scalar, nc.sync])
